import numpy as np, ml_dtypes
CORES = [2,42,66,74,82,90,114]
N = 7
NH, QP = 2, 128
def setup_inputs(rng):
    return {"q": rng.standard_normal((N, 128, NH * QP), dtype=np.float32).astype(ml_dtypes.bfloat16), "k": rng.standard_normal((N, 128, NH * 128), dtype=np.float32).astype(ml_dtypes.bfloat16), "v": rng.standard_normal((N, 128, NH * 128), dtype=np.float32).astype(ml_dtypes.bfloat16)}
def setup_inputs_big(rng):
    d = setup_inputs(rng)
    for k in ("q", "k", "v"): d[k] = (d[k].astype(np.float32) * 1024.0).astype(d[k].dtype)
    return d
def setup_inputs_small(rng):
    d = setup_inputs(rng)
    for k in ("q", "k", "v"): d[k] = (d[k].astype(np.float32) * (1 / 1024.0)).astype(d[k].dtype)
    return d
def setup_inputs_apart(rng):
    d = setup_inputs(rng)
    f = (10.0 ** rng.permutation(np.linspace(-1.5, 1.5, N))).astype(np.float32).reshape(N, 1, 1)
    for k in ("q", "k", "v"): d[k] = (d[k].astype(np.float32) * f).astype(d[k].dtype)
    return d
def reference(q, k, v):
    Q, K, V = q.astype(np.float64), k.astype(np.float64), v.astype(np.float64)
    y = np.zeros((N, 128, NH * QP))
    for r in range(N):
        for h in range(NH):
            for j in range(N):
                S = np.maximum(K[j][:, 128 * h:128 * h + 128].T @ Q[r][:, QP * h:QP * h + QP], 0.0)
                y[r][:, QP * h:QP * h + QP] += V[j][:, 128 * h:128 * h + 128].T @ S
    return {"y": y.astype(ml_dtypes.bfloat16 if q.dtype != np.float64 else np.float64)}

@@ -1,0 +1,282 @@
+from concourse.bass import DstId, RemoteDMATransfer
+from concourse.mybir import AluOpType
+
+N, NH, W = 7, 2, 128
+HW = NH * W
+SLOT = 2 * HW
+NSET = 3
+
+PIECES = [(0, SLOT)]
+STREAMS = [[(0, (0, 1, 2, 3, 4, 5))]]
+HAND_ENG = 8
+DELAY = 2.0
+
+SCRATCH = {
+    "kv": ("sbuf", [128, N * SLOT], "bfloat16"),
+    "qs": ("sbuf", [128, HW], "bfloat16"),
+    "zero": ("sbuf", [128, W], "float32"),
+    "p": ("sbuf", [128, N * HW], "bfloat16"),
+    "ysb": ("sbuf", [128, HW], "bfloat16"),
+    "o0": ("psum", [128, 512], "float32"),
+    "o1": ("psum", [128, 512], "float32"),
+}
+for _i in range(NSET):
+    for _h in range(NH):
+        SCRATCH["s%d_%d" % (_i, _h)] = ("psum", [128, 512], "float32")
+
+SEMAPHORES = ["ld", "ldq", "zs", "sent", "yc0", "yc1", "st0", "st1", "od0", "od1"]
+SEMAPHORES += ["a%d_%d" % (_p, _j) for _p in range(len(PIECES)) for _j in range(N)]
+SEMAPHORES += ["h%d" % _p for _p in range(len(PIECES))]
+SEMAPHORES += ["sd%d_%d" % (_i, _h) for _i in range(N) for _h in range(NH)]
+SEMAPHORES += ["rd%d_%d" % (_i, _h) for _i in range(N) for _h in range(NH)]
+
+_CACHE = {}
+
+
+def _route(topo, s, d):
+    a, b, di = topo.chip(s), topo.chip(d), topo.die(s)
+    if a == b:
+        return []
+    if topo.same_plane(a, b):
+        return [("out", a, di), ("in", b, di)]
+    if topo.mates(a, b):
+        return [("mate", a, di)]
+    m = [x for x in range(topo.CHIPS) if topo.mates(a, x)][0]
+    return [("mate", a, di), ("out", m, di), ("in", b, di)]
+
+
+def _timetable(topo, cores):
+    n = len(cores)
+    for strict in (True, False):
+        used = [set([i]) for i in range(n)]
+        sched = []
+
+        def step(m):
+            if m == n - 1:
+                return True
+            perm = [None] * n
+
+            def place(i, taken, links):
+                if i == n:
+                    sched.append(list(perm))
+                    for s in range(n):
+                        used[s].add(perm[s])
+                    if step(m + 1):
+                        return True
+                    for s in range(n):
+                        used[s].discard(perm[s])
+                    sched.pop()
+                    return False
+                for k in range(1, n):
+                    d = (i + m + k) % n
+                    if d in used[i] or d in taken:
+                        continue
+                    r = _route(topo, cores[i], cores[d])
+                    if strict and any(x in links for x in r):
+                        continue
+                    perm[i] = d
+                    if place(i + 1, taken | set([d]), links | set(r)):
+                        return True
+                return False
+
+            return place(0, set(), set())
+
+        if step(0):
+            return sched
+    return None
+
+
+def _plan(T, topo):
+    if "p" in _CACHE:
+        return _CACHE["p"]
+    cores = list(T.cores)
+    sched = _timetable(topo, cores)
+    role = {}
+    senders = []
+    nhelp = max(w for st in STREAMS for w, _s in st)
+    for r, c in enumerate(cores):
+        others = [d for d in cores if d != c]
+        here = [x for x in range(topo.CHIPS * topo.CORES_PER_CHIP)
+                if topo.chip(x) == topo.chip(c) and x not in cores]
+        far = [x for x in here if topo.die(x) != topo.die(c) and all(topo.may_write(x, d) for d in others)]
+        team = [c] + far[:nhelp]
+        senders.append(team)
+        for w, x in enumerate(team):
+            role[x] = (r, w)
+    when = []
+    for p, (lo, hi) in enumerate(PIECES):
+        frac = (hi - lo) / float(SLOT)
+        tab = [[0.0] * N for _j in range(N)]
+        for w, steps in STREAMS[p]:
+            for pos, m in enumerate(steps):
+                for j in range(N):
+                    tab[j][sched[m][j]] = (DELAY if w else 0.0) + (pos + 1) * frac
+        when.append(tab)
+    _CACHE["p"] = {"cores": cores, "sched": sched, "role": role, "senders": senders, "when": when}
+    return _CACHE["p"]
+
+
+def _pick(mask, n):
+    out, got, b = 0, 0, 0
+    while got < n:
+        if (mask >> b) & 1:
+            out |= 1 << b
+            got += 1
+        b += 1
+    return out
+
+
+def _count(mask):
+    return bin(mask).count("1")
+
+
+def _groups(n):
+    out = []
+    while n:
+        k = (n + 1) // 2
+        out.append(k)
+        n -= k
+    return out
+
+
+def _transfer(T, topo, cols, dests, sem, mask):
+    ids = []
+    for d in dests:
+        a = topo.addr(d)
+        ids.append(DstId(rid=a[0], pnc=a[1]))
+    ap = T.kv[:, cols[0]:cols[1]]
+    return RemoteDMATransfer(dst_ids=ids, dma_engine_mask=mask, remote_sem=sem, srcs=[ap],
+                             dsts=[ap for _d in dests], alu_op=0)
+
+
+def _away_mask(topo, core, cores):
+    m = None
+    for d in cores:
+        if d != core:
+            m = topo.mask(core, d) if m is None else (m & topo.mask(core, d))
+    return m
+
+
+def _send(g, core, T, topo, P, r, who):
+    cores, sched, team = P["cores"], P["sched"], P["senders"][r]
+    base = r * SLOT
+    away = _away_mask(topo, core, [c for c in cores if c != cores[r]])
+    handed = [p for p in range(len(PIECES)) if any(w for w, _s in STREAMS[p])]
+    each = HAND_ENG // max(1, len(handed))
+    first, calls, total = [], [], 0
+    if who == 0:
+        g.wait_ge(T.sem.ld, 32)
+        for n, p in enumerate(handed):
+            hs = [team[w] for w, _s in STREAMS[p] if w]
+            spare = ~away
+            for x in hs:
+                spare &= topo.mask(core, x)
+            m = _pick(spare, each * (n + 1)) & ~_pick(spare, each * n)
+            first.append(_transfer(T, topo, (base + PIECES[p][0], base + PIECES[p][1]), hs, T.sem["h%d" % p], m))
+            total += each
+    for p, (lo, hi) in enumerate(PIECES):
+        for w, steps in STREAMS[p]:
+            if w != who:
+                continue
+            if who:
+                g.wait_ge(T.sem["h%d" % p], each)
+            at = 0
+            for k in _groups(len(steps)):
+                dests = [cores[sched[m][r]] for m in steps[at:at + k]]
+                at += k
+                calls.append([_transfer(T, topo, (base + lo, base + hi), dests, T.sem["a%d_%d" % (p, r)], away)])
+                total += _count(away)
+    if first and calls:
+        calls[0] = first + calls[0]
+    elif first:
+        calls = [first]
+    for trs in calls:
+        g.remote_dma_fused(trs, local_sem=T.sem.sent)
+    g.wait_ge(T.sem.sent, total)
+
+
+def _compute(g, core, T, topo, P, r):
+    sem = T.sem
+    when = P["when"]
+    cnt = _count(_away_mask(topo, core, P["cores"]))
+    kp = [p for p, (lo, hi) in enumerate(PIECES) if lo < HW]
+    vp = [p for p, (lo, hi) in enumerate(PIECES) if hi > HW]
+    tk = [max(when[p][j][r] for p in kp) for j in range(N)]
+    tv = [max(tk[j], max(when[p][j][r] for p in vp)) for j in range(N)]
+    sorder = sorted(range(N), key=lambda j: (tk[j], j != r))
+    spos = dict((j, i) for i, j in enumerate(sorder))
+    last = tk[sorder[-1]]
+    lag = 1.1 * (PIECES[kp[0]][1] - PIECES[kp[0]][0]) / float(SLOT)
+    ops = [(tk[j], 0, spos[j], j) for j in range(N)]
+    for j in range(N):
+        t = tv[j] + lag
+        if tv[j] < last:
+            t = min(t, last - 0.01)
+        ops.append((t, 1, spos[j], j))
+    ops.sort()
+
+    base = r * SLOT
+    g.sync.dma_start(T.kv[:, base:base + HW], T.k[:, :]).then_inc(sem.ld, 16)
+    g.scalar.dma_start(T.kv[:, base + HW:base + SLOT], T.v[:, :]).then_inc(sem.ld, 16)
+    g.sync.dma_start(T.qs[:, :], T.q[:, :]).then_inc(sem.ldq, 16)
+
+    waited = set()
+
+    def tw(name, val):
+        if name not in waited:
+            g.tensor.wait_ge(sem[name], val)
+            waited.add(name)
+
+    tw("ld", 32)
+    tw("ldq", 16)
+    done = 0
+    for _t, kind, i, j in ops:
+        if kind == 0:
+            if j != r:
+                for p in kp:
+                    tw("a%d_%d" % (p, j), cnt)
+            for h in range(NH):
+                if i >= NSET:
+                    tw("rd%d_%d" % (i - NSET, h), 1)
+                g.tensor.matmul(T["s%d_%d" % (i % NSET, h)][:, 0:W], T.kv[:, j * SLOT + h * W:j * SLOT + (h + 1) * W],
+                                T.qs[:, h * W:(h + 1) * W], start=True, stop=True).then_inc(sem["sd%d_%d" % (i, h)], 1)
+        else:
+            if j != r:
+                for p in vp:
+                    tw("a%d_%d" % (p, j), cnt)
+            for h in range(NH):
+                tw("rd%d_%d" % (i, h), 1)
+                mm = g.tensor.matmul(T["o%d" % h][:, 0:W],
+                                     T.kv[:, j * SLOT + HW + h * W:j * SLOT + HW + (h + 1) * W],
+                                     T.p[:, (i * NH + h) * W:(i * NH + h + 1) * W],
+                                     start=(done == 0), stop=(done == N - 1))
+                if done == N - 1:
+                    mm.then_inc(sem["od%d" % h], 1)
+            done += 1
+
+    g.vector.memset(T.zero[:, :], 0.0).then_inc(sem.zs, 1)
+    g.vector.wait_ge(sem.zs, 1)
+    for i in range(N):
+        for h in range(NH):
+            g.vector.wait_ge(sem["sd%d_%d" % (i, h)], 1)
+            g.vector.tensor_tensor(T.p[:, (i * NH + h) * W:(i * NH + h + 1) * W], T["s%d_%d" % (i % NSET, h)][:, 0:W],
+                                   T.zero[:, :], AluOpType.max).then_inc(sem["rd%d_%d" % (i, h)], 1)
+    for h in range(NH):
+        g.vector.wait_ge(sem["od%d" % h], 1)
+        g.vector.tensor_copy(T.ysb[:, h * W:(h + 1) * W], T["o%d" % h][:, 0:W]).then_inc(sem["yc%d" % h], 1)
+
+    for h, qu in enumerate((g.sync, g.scalar)):
+        qu.wait_ge(sem["yc%d" % h], 1)
+        qu.dma_start(T.y[:, h * W:(h + 1) * W], T.ysb[:, h * W:(h + 1) * W]).then_inc(sem["st%d" % h], 16)
+        qu.wait_ge(sem["st%d" % h], 16)
+
+
+def rank_program(g, core, T, topo):
+    P = _plan(T, topo)
+    role = P["role"].get(core)
+    if role is None:
+        return
+    r, who = role
+    if who == 0:
+        _compute(g, core, T, topo, P, r)
+    _send(g, core, T, topo, P, r, who)

@@ -6,8 +6,8 @@ HW = NH * W
 SLOT = 2 * HW
 NSET = 3
 
-PIECES = [(0, SLOT)]
-STREAMS = [[(0, (0, 1, 2, 3, 4, 5))]]
+PIECES = [(0, HW), (HW, SLOT)]
+STREAMS = [[(0, (0, 1, 2, 3, 4, 5))], [(1, (0, 1, 2)), (2, (3, 4, 5))]]
 HAND_ENG = 8
 DELAY = 2.0
 

from concourse.bass import DstId, RemoteDMATransfer
from concourse.mybir import AluOpType

N, NH, W = 7, 2, 128
HW = NH * W
SLOT = 2 * HW
NSET = 3

PIECES = [(0, HW), (HW, SLOT)]
STREAMS = [[(0, (0, 1, 2, 3, 4, 5))], [(1, (0, 1, 2)), (2, (3, 4, 5))]]
HAND_ENG = 8
DELAY = 2.0

SCRATCH = {
    "kv": ("sbuf", [128, N * SLOT], "bfloat16"),
    "qs": ("sbuf", [128, HW], "bfloat16"),
    "zero": ("sbuf", [128, W], "float32"),
    "p": ("sbuf", [128, N * HW], "bfloat16"),
    "ysb": ("sbuf", [128, HW], "bfloat16"),
    "o0": ("psum", [128, 512], "float32"),
    "o1": ("psum", [128, 512], "float32"),
}
for _i in range(NSET):
    for _h in range(NH):
        SCRATCH["s%d_%d" % (_i, _h)] = ("psum", [128, 512], "float32")

SEMAPHORES = ["ld", "ldq", "zs", "sent", "yc0", "yc1", "st0", "st1", "od0", "od1"]
SEMAPHORES += ["a%d_%d" % (_p, _j) for _p in range(len(PIECES)) for _j in range(N)]
SEMAPHORES += ["h%d" % _p for _p in range(len(PIECES))]
SEMAPHORES += ["sd%d_%d" % (_i, _h) for _i in range(N) for _h in range(NH)]
SEMAPHORES += ["rd%d_%d" % (_i, _h) for _i in range(N) for _h in range(NH)]

_CACHE = {}


def _route(topo, s, d):
    a, b, di = topo.chip(s), topo.chip(d), topo.die(s)
    if a == b:
        return []
    if topo.same_plane(a, b):
        return [("out", a, di), ("in", b, di)]
    if topo.mates(a, b):
        return [("mate", a, di)]
    m = [x for x in range(topo.CHIPS) if topo.mates(a, x)][0]
    return [("mate", a, di), ("out", m, di), ("in", b, di)]


def _timetable(topo, cores):
    n = len(cores)
    for strict in (True, False):
        used = [set([i]) for i in range(n)]
        sched = []

        def step(m):
            if m == n - 1:
                return True
            perm = [None] * n

            def place(i, taken, links):
                if i == n:
                    sched.append(list(perm))
                    for s in range(n):
                        used[s].add(perm[s])
                    if step(m + 1):
                        return True
                    for s in range(n):
                        used[s].discard(perm[s])
                    sched.pop()
                    return False
                for k in range(1, n):
                    d = (i + m + k) % n
                    if d in used[i] or d in taken:
                        continue
                    r = _route(topo, cores[i], cores[d])
                    if strict and any(x in links for x in r):
                        continue
                    perm[i] = d
                    if place(i + 1, taken | set([d]), links | set(r)):
                        return True
                return False

            return place(0, set(), set())

        if step(0):
            return sched
    return None


def _plan(T, topo):
    if "p" in _CACHE:
        return _CACHE["p"]
    cores = list(T.cores)
    sched = _timetable(topo, cores)
    role = {}
    senders = []
    nhelp = max(w for st in STREAMS for w, _s in st)
    for r, c in enumerate(cores):
        others = [d for d in cores if d != c]
        here = [x for x in range(topo.CHIPS * topo.CORES_PER_CHIP)
                if topo.chip(x) == topo.chip(c) and x not in cores]
        far = [x for x in here if topo.die(x) != topo.die(c) and all(topo.may_write(x, d) for d in others)]
        team = [c] + far[:nhelp]
        senders.append(team)
        for w, x in enumerate(team):
            role[x] = (r, w)
    when = []
    for p, (lo, hi) in enumerate(PIECES):
        frac = (hi - lo) / float(SLOT)
        tab = [[0.0] * N for _j in range(N)]
        for w, steps in STREAMS[p]:
            for pos, m in enumerate(steps):
                for j in range(N):
                    tab[j][sched[m][j]] = (DELAY if w else 0.0) + (pos + 1) * frac
        when.append(tab)
    _CACHE["p"] = {"cores": cores, "sched": sched, "role": role, "senders": senders, "when": when}
    return _CACHE["p"]


def _pick(mask, n):
    out, got, b = 0, 0, 0
    while got < n:
        if (mask >> b) & 1:
            out |= 1 << b
            got += 1
        b += 1
    return out


def _count(mask):
    return bin(mask).count("1")


def _groups(n):
    out = []
    while n:
        k = (n + 1) // 2
        out.append(k)
        n -= k
    return out


def _transfer(T, topo, cols, dests, sem, mask):
    ids = []
    for d in dests:
        a = topo.addr(d)
        ids.append(DstId(rid=a[0], pnc=a[1]))
    ap = T.kv[:, cols[0]:cols[1]]
    return RemoteDMATransfer(dst_ids=ids, dma_engine_mask=mask, remote_sem=sem, srcs=[ap],
                             dsts=[ap for _d in dests], alu_op=0)


def _away_mask(topo, core, cores):
    m = None
    for d in cores:
        if d != core:
            m = topo.mask(core, d) if m is None else (m & topo.mask(core, d))
    return m


def _send(g, core, T, topo, P, r, who):
    cores, sched, team = P["cores"], P["sched"], P["senders"][r]
    base = r * SLOT
    away = _away_mask(topo, core, [c for c in cores if c != cores[r]])
    handed = [p for p in range(len(PIECES)) if any(w for w, _s in STREAMS[p])]
    each = HAND_ENG // max(1, len(handed))
    first, calls, total = [], [], 0
    if who == 0:
        g.wait_ge(T.sem.ld, 32)
        for n, p in enumerate(handed):
            hs = [team[w] for w, _s in STREAMS[p] if w]
            spare = ~away
            for x in hs:
                spare &= topo.mask(core, x)
            m = _pick(spare, each * (n + 1)) & ~_pick(spare, each * n)
            first.append(_transfer(T, topo, (base + PIECES[p][0], base + PIECES[p][1]), hs, T.sem["h%d" % p], m))
            total += each
    for p, (lo, hi) in enumerate(PIECES):
        for w, steps in STREAMS[p]:
            if w != who:
                continue
            if who:
                g.wait_ge(T.sem["h%d" % p], each)
            at = 0
            for k in _groups(len(steps)):
                dests = [cores[sched[m][r]] for m in steps[at:at + k]]
                at += k
                calls.append([_transfer(T, topo, (base + lo, base + hi), dests, T.sem["a%d_%d" % (p, r)], away)])
                total += _count(away)
    if first and calls:
        calls[0] = first + calls[0]
    elif first:
        calls = [first]
    for trs in calls:
        g.remote_dma_fused(trs, local_sem=T.sem.sent)
    g.wait_ge(T.sem.sent, total)


def _compute(g, core, T, topo, P, r):
    sem = T.sem
    when = P["when"]
    cnt = _count(_away_mask(topo, core, P["cores"]))
    kp = [p for p, (lo, hi) in enumerate(PIECES) if lo < HW]
    vp = [p for p, (lo, hi) in enumerate(PIECES) if hi > HW]
    tk = [max(when[p][j][r] for p in kp) for j in range(N)]
    tv = [max(tk[j], max(when[p][j][r] for p in vp)) for j in range(N)]
    sorder = sorted(range(N), key=lambda j: (tk[j], j != r))
    spos = dict((j, i) for i, j in enumerate(sorder))
    last = tk[sorder[-1]]
    lag = 1.1 * (PIECES[kp[0]][1] - PIECES[kp[0]][0]) / float(SLOT)
    ops = [(tk[j], 0, spos[j], j) for j in range(N)]
    for j in range(N):
        t = tv[j] + lag
        if tv[j] < last:
            t = min(t, last - 0.01)
        ops.append((t, 1, spos[j], j))
    ops.sort()

    base = r * SLOT
    g.sync.dma_start(T.kv[:, base:base + HW], T.k[:, :]).then_inc(sem.ld, 16)
    g.scalar.dma_start(T.kv[:, base + HW:base + SLOT], T.v[:, :]).then_inc(sem.ld, 16)
    g.sync.dma_start(T.qs[:, :], T.q[:, :]).then_inc(sem.ldq, 16)

    waited = set()

    def tw(name, val):
        if name not in waited:
            g.tensor.wait_ge(sem[name], val)
            waited.add(name)

    tw("ld", 32)
    tw("ldq", 16)
    done = 0
    for _t, kind, i, j in ops:
        if kind == 0:
            if j != r:
                for p in kp:
                    tw("a%d_%d" % (p, j), cnt)
            for h in range(NH):
                if i >= NSET:
                    tw("rd%d_%d" % (i - NSET, h), 1)
                g.tensor.matmul(T["s%d_%d" % (i % NSET, h)][:, 0:W], T.kv[:, j * SLOT + h * W:j * SLOT + (h + 1) * W],
                                T.qs[:, h * W:(h + 1) * W], start=True, stop=True).then_inc(sem["sd%d_%d" % (i, h)], 1)
        else:
            if j != r:
                for p in vp:
                    tw("a%d_%d" % (p, j), cnt)
            for h in range(NH):
                tw("rd%d_%d" % (i, h), 1)
                mm = g.tensor.matmul(T["o%d" % h][:, 0:W],
                                     T.kv[:, j * SLOT + HW + h * W:j * SLOT + HW + (h + 1) * W],
                                     T.p[:, (i * NH + h) * W:(i * NH + h + 1) * W],
                                     start=(done == 0), stop=(done == N - 1))
                if done == N - 1:
                    mm.then_inc(sem["od%d" % h], 1)
            done += 1

    g.vector.memset(T.zero[:, :], 0.0).then_inc(sem.zs, 1)
    g.vector.wait_ge(sem.zs, 1)
    for i in range(N):
        for h in range(NH):
            g.vector.wait_ge(sem["sd%d_%d" % (i, h)], 1)
            g.vector.tensor_tensor(T.p[:, (i * NH + h) * W:(i * NH + h + 1) * W], T["s%d_%d" % (i % NSET, h)][:, 0:W],
                                   T.zero[:, :], AluOpType.max).then_inc(sem["rd%d_%d" % (i, h)], 1)
    for h in range(NH):
        g.vector.wait_ge(sem["od%d" % h], 1)
        g.vector.tensor_copy(T.ysb[:, h * W:(h + 1) * W], T["o%d" % h][:, 0:W]).then_inc(sem["yc%d" % h], 1)

    for h, qu in enumerate((g.sync, g.scalar)):
        qu.wait_ge(sem["yc%d" % h], 1)
        qu.dma_start(T.y[:, h * W:(h + 1) * W], T.ysb[:, h * W:(h + 1) * W]).then_inc(sem["st%d" % h], 16)
        qu.wait_ge(sem["st%d" % h], 16)


def rank_program(g, core, T, topo):
    P = _plan(T, topo)
    role = P["role"].get(core)
    if role is None:
        return
    r, who = role
    if who == 0:
        _compute(g, core, T, topo, P, r)
    _send(g, core, T, topo, P, r, who)
